import numpy as np
import ml_dtypes

BF16 = ml_dtypes.bfloat16


def bf(x):
    return np.asarray(x, np.float32).astype(BF16)


def f32(x):
    return np.asarray(x, np.float32)


def f64(x):
    return np.asarray(x).astype(np.float64)


def striped(idx):
    return np.tile(idx.reshape(-1, 16).T, (8, 1))


S, K, M, N, D, V = 1024, 256, 256, 384, 2, 192


def setup_inputs():
    return {"table": bf(np.random.standard_normal((K, S))), "w": bf(np.random.standard_normal((K, M)) / np.sqrt(D * K)), "c": f32(0.2 + 0.8 * np.random.random_sample((1, V))), "offs": striped(np.random.permutation(np.tile(np.arange(S), 2))[:N])}


def reference(table, w, c, offs):
    idx = offs[:16].T.reshape(-1)
    x = f64(table)[:, idx]
    y = f64(w).T @ sum(x[:, t * V : (t + 1) * V] for t in range(D))
    return y * f64(c)

@@ -1,0 +1,56 @@
+import concourse.mybir as mybir
+
+BF16 = mybir.dt.bfloat16
+F32 = mybir.dt.float32
+U16 = mybir.dt.uint16
+
+P = 128
+S = 1024
+K = 256
+M = 256
+V = 192
+D = 2
+N = D * V
+K_BLOCKS = K // P
+M_BLOCKS = M // P
+PIECE_COLUMNS = V // 16
+
+FLOPS = 2 * K * M * V + (D - 1) * K * V + M * V
+BYTES = 2 * K * N + 2 * K * M + 4 * V + 2 * N + 4 * M * V
+
+
+def tile_gather_matmul_kernel(tc, table, w, c, offs, out):
+    nc = tc.nc
+    with (
+        tc.tile_pool(name="held", bufs=1) as held,
+        tc.tile_pool(name="results", bufs=2) as results,
+        tc.psum_pool(name="banks", bufs=2) as banks,
+    ):
+        offsets = held.tile([P, N // 16], U16, name="offsets")
+        nc.sync.dma_start(offsets[:], offs)
+
+        table_blocks = [held.tile([P, S], BF16, name=f"table{k}") for k in range(K_BLOCKS)]
+        w_blocks = [held.tile([P, M], BF16, name=f"w{k}") for k in range(K_BLOCKS)]
+        queues = [nc.sync, nc.scalar]
+        for k in range(K_BLOCKS):
+            queues[k].dma_start(w_blocks[k][:], w[k * P : (k + 1) * P, :])
+            queues[k].dma_start(table_blocks[k][:], table[k * P : (k + 1) * P, :])
+
+        c_rows = held.tile([P, V], F32, name="c_rows")
+        nc.gpsimd.dma_start(c_rows[:], c.to_broadcast([P, V]))
+
+        for m in range(M_BLOCKS):
+            bank = banks.tile([P, V], F32, name="bank")
+            steps = [(k, t) for k in range(K_BLOCKS) for t in range(D)]
+            for step, (k, t) in enumerate(steps):
+                piece = offsets[:, t * PIECE_COLUMNS : (t + 1) * PIECE_COLUMNS]
+                nc.tensor.matmul(
+                    bank[:],
+                    w_blocks[k][:, m * P : (m + 1) * P],
+                    table_blocks[k][:].indirect(piece),
+                    start=(step == 0),
+                    stop=(step == len(steps) - 1),
+                )
+            result = results.tile([P, V], F32, name="result")
+            nc.vector.tensor_tensor(result[:], bank[:], c_rows[:], mybir.AluOpType.mult)
+            queues[m].dma_start(out[m * P : (m + 1) * P, :], result[:])

@@ -23,34 +23,35 @@ def tile_gather_matmul_kernel(tc, table, w, c, offs, out):
     nc = tc.nc
     with (
         tc.tile_pool(name="held", bufs=1) as held,
-        tc.tile_pool(name="results", bufs=2) as results,
-        tc.psum_pool(name="banks", bufs=2) as banks,
+        tc.psum_pool(name="banks", bufs=1) as banks,
     ):
         offsets = held.tile([P, N // 16], U16, name="offsets")
         nc.sync.dma_start(offsets[:], offs)
 
         table_blocks = [held.tile([P, S], BF16, name=f"table{k}") for k in range(K_BLOCKS)]
         w_blocks = [held.tile([P, M], BF16, name=f"w{k}") for k in range(K_BLOCKS)]
-        queues = [nc.sync, nc.scalar]
         for k in range(K_BLOCKS):
-            queues[k].dma_start(w_blocks[k][:], w[k * P : (k + 1) * P, :])
-            queues[k].dma_start(table_blocks[k][:], table[k * P : (k + 1) * P, :])
+            nc.sync.dma_start(table_blocks[k][:], table[k * P : (k + 1) * P, :])
+            nc.scalar.dma_start(w_blocks[k][:], w[k * P : (k + 1) * P, :])
 
         c_rows = held.tile([P, V], F32, name="c_rows")
         nc.gpsimd.dma_start(c_rows[:], c.to_broadcast([P, V]))
 
+        bank_of = [banks.tile([P, V], F32, name=f"bank{m}") for m in range(M_BLOCKS)]
+        for k in range(K_BLOCKS):
+            for m in range(M_BLOCKS):
+                for t in range(D):
+                    piece = offsets[:, t * PIECE_COLUMNS : (t + 1) * PIECE_COLUMNS]
+                    nc.tensor.matmul(
+                        bank_of[m][:],
+                        w_blocks[k][:, m * P : (m + 1) * P],
+                        table_blocks[k][:].indirect(piece),
+                        start=(k == 0 and t == 0),
+                        stop=(k == K_BLOCKS - 1 and t == D - 1),
+                    )
+
+        store_queues = [nc.sync, nc.scalar]
         for m in range(M_BLOCKS):
-            bank = banks.tile([P, V], F32, name="bank")
-            steps = [(k, t) for k in range(K_BLOCKS) for t in range(D)]
-            for step, (k, t) in enumerate(steps):
-                piece = offsets[:, t * PIECE_COLUMNS : (t + 1) * PIECE_COLUMNS]
-                nc.tensor.matmul(
-                    bank[:],
-                    w_blocks[k][:, m * P : (m + 1) * P],
-                    table_blocks[k][:].indirect(piece),
-                    start=(step == 0),
-                    stop=(step == len(steps) - 1),
-                )
-            result = results.tile([P, V], F32, name="result")
-            nc.vector.tensor_tensor(result[:], bank[:], c_rows[:], mybir.AluOpType.mult)
-            queues[m].dma_start(out[m * P : (m + 1) * P, :], result[:])
+            result = held.tile([P, V], F32, name=f"result{m}")
+            nc.vector.tensor_tensor(result[:], bank_of[m][:], c_rows[:], mybir.AluOpType.mult)
+            store_queues[m].dma_start(out[m * P : (m + 1) * P, :], result[:])

@@ -28,14 +28,21 @@ def tile_gather_matmul_kernel(tc, table, w, c, offs, out):
         offsets = held.tile([P, N // 16], U16, name="offsets")
         nc.sync.dma_start(offsets[:], offs)
 
+        c_row = held.tile([1, V], F32, name="c_row")
+        nc.scalar.dma_start(c_row[:], c)
+
         table_blocks = [held.tile([P, S], BF16, name=f"table{k}") for k in range(K_BLOCKS)]
         w_blocks = [held.tile([P, M], BF16, name=f"w{k}") for k in range(K_BLOCKS)]
         for k in range(K_BLOCKS):
             nc.sync.dma_start(table_blocks[k][:], table[k * P : (k + 1) * P, :])
             nc.scalar.dma_start(w_blocks[k][:], w[k * P : (k + 1) * P, :])
 
+        ones = held.tile([1, P], F32, name="ones")
+        nc.vector.memset(ones[:], 1.0)
+        c_bank = banks.tile([P, V], F32, name="c_bank")
+        nc.tensor.matmul(c_bank[:], ones[:], c_row[:], start=True, stop=True)
         c_rows = held.tile([P, V], F32, name="c_rows")
-        nc.gpsimd.dma_start(c_rows[:], c.to_broadcast([P, V]))
+        nc.vector.tensor_copy(c_rows[:], c_bank[:])
 
         bank_of = [banks.tile([P, V], F32, name=f"bank{m}") for m in range(M_BLOCKS)]
         for k in range(K_BLOCKS):

@@ -14,6 +14,7 @@ N = D * V
 K_BLOCKS = K // P
 M_BLOCKS = M // P
 PIECE_COLUMNS = V // 16
+WARM_MATMULS = 16
 
 FLOPS = 2 * K * M * V + (D - 1) * K * V + M * V
 BYTES = 2 * K * N + 2 * K * M + 4 * V + 2 * N + 4 * M * V
@@ -36,6 +37,12 @@ def tile_gather_matmul_kernel(tc, table, w, c, offs, out):
         for k in range(K_BLOCKS):
             nc.sync.dma_start(table_blocks[k][:], table[k * P : (k + 1) * P, :])
             nc.scalar.dma_start(w_blocks[k][:], w[k * P : (k + 1) * P, :])
+
+        zeros = held.tile([P, P], BF16, name="zeros")
+        nc.vector.memset(zeros[:], 0.0)
+        warm_bank = banks.tile([P, P], F32, name="warm_bank")
+        for i in range(WARM_MATMULS):
+            nc.tensor.matmul(warm_bank[:], zeros[:], zeros[:], start=True, stop=True)
 
         ones = held.tile([1, P], F32, name="ones")
         nc.vector.memset(ones[:], 1.0)

@@ -14,7 +14,6 @@ N = D * V
 K_BLOCKS = K // P
 M_BLOCKS = M // P
 PIECE_COLUMNS = V // 16
-WARM_MATMULS = 16
 
 FLOPS = 2 * K * M * V + (D - 1) * K * V + M * V
 BYTES = 2 * K * N + 2 * K * M + 4 * V + 2 * N + 4 * M * V
@@ -38,12 +37,6 @@ def tile_gather_matmul_kernel(tc, table, w, c, offs, out):
             nc.sync.dma_start(table_blocks[k][:], table[k * P : (k + 1) * P, :])
             nc.scalar.dma_start(w_blocks[k][:], w[k * P : (k + 1) * P, :])
 
-        zeros = held.tile([P, P], BF16, name="zeros")
-        nc.vector.memset(zeros[:], 0.0)
-        warm_bank = banks.tile([P, P], F32, name="warm_bank")
-        for i in range(WARM_MATMULS):
-            nc.tensor.matmul(warm_bank[:], zeros[:], zeros[:], start=True, stop=True)
-
         ones = held.tile([1, P], F32, name="ones")
         nc.vector.memset(ones[:], 1.0)
         c_bank = banks.tile([P, V], F32, name="c_bank")
@@ -51,21 +44,19 @@ def tile_gather_matmul_kernel(tc, table, w, c, offs, out):
         c_rows = held.tile([P, V], F32, name="c_rows")
         nc.vector.tensor_copy(c_rows[:], c_bank[:])
 
-        bank_of = [banks.tile([P, V], F32, name=f"bank{m}") for m in range(M_BLOCKS)]
-        for k in range(K_BLOCKS):
-            for m in range(M_BLOCKS):
+        store_queues = [nc.sync, nc.scalar]
+        for m in range(M_BLOCKS):
+            bank = banks.tile([P, V], F32, name=f"bank{m}")
+            for k in range(K_BLOCKS):
                 for t in range(D):
                     piece = offsets[:, t * PIECE_COLUMNS : (t + 1) * PIECE_COLUMNS]
                     nc.tensor.matmul(
-                        bank_of[m][:],
+                        bank[:],
                         w_blocks[k][:, m * P : (m + 1) * P],
                         table_blocks[k][:].indirect(piece),
                         start=(k == 0 and t == 0),
                         stop=(k == K_BLOCKS - 1 and t == D - 1),
                     )
-
-        store_queues = [nc.sync, nc.scalar]
-        for m in range(M_BLOCKS):
             result = held.tile([P, V], F32, name=f"result{m}")
-            nc.vector.tensor_tensor(result[:], bank_of[m][:], c_rows[:], mybir.AluOpType.mult)
+            nc.vector.tensor_tensor(result[:], bank[:], c_rows[:], mybir.AluOpType.mult)
             store_queues[m].dma_start(out[m * P : (m + 1) * P, :], result[:])

@@ -44,7 +44,6 @@ def tile_gather_matmul_kernel(tc, table, w, c, offs, out):
         c_rows = held.tile([P, V], F32, name="c_rows")
         nc.vector.tensor_copy(c_rows[:], c_bank[:])
 
-        store_queues = [nc.sync, nc.scalar]
         for m in range(M_BLOCKS):
             bank = banks.tile([P, V], F32, name=f"bank{m}")
             for k in range(K_BLOCKS):
@@ -59,4 +58,4 @@ def tile_gather_matmul_kernel(tc, table, w, c, offs, out):
                     )
             result = held.tile([P, V], F32, name=f"result{m}")
             nc.vector.tensor_tensor(result[:], bank[:], c_rows[:], mybir.AluOpType.mult)
-            store_queues[m].dma_start(out[m * P : (m + 1) * P, :], result[:])
+            nc.scalar.dma_start(out[m * P : (m + 1) * P, :], result[:])

@@ -14,6 +14,7 @@ N = D * V
 K_BLOCKS = K // P
 M_BLOCKS = M // P
 PIECE_COLUMNS = V // 16
+WARM_MATMULS = 8
 
 FLOPS = 2 * K * M * V + (D - 1) * K * V + M * V
 BYTES = 2 * K * N + 2 * K * M + 4 * V + 2 * N + 4 * M * V
@@ -36,6 +37,12 @@ def tile_gather_matmul_kernel(tc, table, w, c, offs, out):
         for k in range(K_BLOCKS):
             nc.sync.dma_start(table_blocks[k][:], table[k * P : (k + 1) * P, :])
             nc.scalar.dma_start(w_blocks[k][:], w[k * P : (k + 1) * P, :])
+
+        zeros = held.tile([P, P], BF16, name="zeros")
+        nc.vector.memset(zeros[:], 0.0)
+        warm_bank = banks.tile([P, P], F32, name="warm_bank")
+        for repeat in range(WARM_MATMULS):
+            nc.tensor.matmul(warm_bank[:], zeros[:], zeros[:], start=True, stop=True)
 
         ones = held.tile([1, P], F32, name="ones")
         nc.vector.memset(ones[:], 1.0)

@@ -44,10 +44,14 @@ def tile_gather_matmul_kernel(tc, table, w, c, offs, out):
         for repeat in range(WARM_MATMULS):
             nc.tensor.matmul(warm_bank[:], zeros[:], zeros[:], start=True, stop=True)
 
-        ones = held.tile([1, P], F32, name="ones")
+        ones = held.tile([1, P], BF16, name="ones")
         nc.vector.memset(ones[:], 1.0)
+        c_upper = c_row[:].bitcast(BF16).rearrange("o (v h) -> o v h", h=2)[:, :, 1]
+        c_rest = held.tile([1, V], BF16, name="c_rest")
+        nc.vector.tensor_tensor(c_rest[:], c_row[:], c_upper, mybir.AluOpType.subtract)
         c_bank = banks.tile([P, V], F32, name="c_bank")
-        nc.tensor.matmul(c_bank[:], ones[:], c_row[:], start=True, stop=True)
+        nc.tensor.matmul(c_bank[:], ones[:], c_upper, start=True, stop=False)
+        nc.tensor.matmul(c_bank[:], ones[:], c_rest[:], start=False, stop=True)
         c_rows = held.tile([P, V], F32, name="c_rows")
         nc.vector.tensor_copy(c_rows[:], c_bank[:])
 

import concourse.mybir as mybir

BF16 = mybir.dt.bfloat16
F32 = mybir.dt.float32
U16 = mybir.dt.uint16

P = 128
S = 1024
K = 256
M = 256
V = 192
D = 2
N = D * V
K_BLOCKS = K // P
M_BLOCKS = M // P
PIECE_COLUMNS = V // 16
WARM_MATMULS = 8

FLOPS = 2 * K * M * V + (D - 1) * K * V + M * V
BYTES = 2 * K * N + 2 * K * M + 4 * V + 2 * N + 4 * M * V


def tile_gather_matmul_kernel(tc, table, w, c, offs, out):
    nc = tc.nc
    with (
        tc.tile_pool(name="held", bufs=1) as held,
        tc.psum_pool(name="banks", bufs=1) as banks,
    ):
        offsets = held.tile([P, N // 16], U16, name="offsets")
        nc.sync.dma_start(offsets[:], offs)

        c_row = held.tile([1, V], F32, name="c_row")
        nc.scalar.dma_start(c_row[:], c)

        table_blocks = [held.tile([P, S], BF16, name=f"table{k}") for k in range(K_BLOCKS)]
        w_blocks = [held.tile([P, M], BF16, name=f"w{k}") for k in range(K_BLOCKS)]
        for k in range(K_BLOCKS):
            nc.sync.dma_start(table_blocks[k][:], table[k * P : (k + 1) * P, :])
            nc.scalar.dma_start(w_blocks[k][:], w[k * P : (k + 1) * P, :])

        zeros = held.tile([P, P], BF16, name="zeros")
        nc.vector.memset(zeros[:], 0.0)
        warm_bank = banks.tile([P, P], F32, name="warm_bank")
        for repeat in range(WARM_MATMULS):
            nc.tensor.matmul(warm_bank[:], zeros[:], zeros[:], start=True, stop=True)

        ones = held.tile([1, P], BF16, name="ones")
        nc.vector.memset(ones[:], 1.0)
        c_upper = c_row[:].bitcast(BF16).rearrange("o (v h) -> o v h", h=2)[:, :, 1]
        c_rest = held.tile([1, V], BF16, name="c_rest")
        nc.vector.tensor_tensor(c_rest[:], c_row[:], c_upper, mybir.AluOpType.subtract)
        c_bank = banks.tile([P, V], F32, name="c_bank")
        nc.tensor.matmul(c_bank[:], ones[:], c_upper, start=True, stop=False)
        nc.tensor.matmul(c_bank[:], ones[:], c_rest[:], start=False, stop=True)
        c_rows = held.tile([P, V], F32, name="c_rows")
        nc.vector.tensor_copy(c_rows[:], c_bank[:])

        for m in range(M_BLOCKS):
            bank = banks.tile([P, V], F32, name=f"bank{m}")
            for k in range(K_BLOCKS):
                for t in range(D):
                    piece = offsets[:, t * PIECE_COLUMNS : (t + 1) * PIECE_COLUMNS]
                    nc.tensor.matmul(
                        bank[:],
                        w_blocks[k][:, m * P : (m + 1) * P],
                        table_blocks[k][:].indirect(piece),
                        start=(k == 0 and t == 0),
                        stop=(k == K_BLOCKS - 1 and t == D - 1),
                    )
            result = held.tile([P, V], F32, name=f"result{m}")
            nc.vector.tensor_tensor(result[:], bank[:], c_rows[:], mybir.AluOpType.mult)
            nc.scalar.dma_start(out[m * P : (m + 1) * P, :], result[:])
